import numpy as np
import ml_dtypes


def mxq(x, axis, fmt="e4m3"):
    dtype, down = {"e4m3": (ml_dtypes.float8_e4m3fn, 7), "e5m2": (ml_dtypes.float8_e5m2, 14)}[fmt]
    v = np.moveaxis(np.asarray(x, np.float32).astype(ml_dtypes.bfloat16).astype(np.float64), axis, -1)
    blocks = v.reshape(v.shape[:-1] + (-1, 32))
    amax = np.abs(blocks).max(-1, keepdims=True)
    byte = np.maximum(np.where(amax > 0, np.frexp(amax)[1] - 1 + 127, 0) - down, 1)
    scale = np.exp2(byte - 127.0)
    codes = (blocks / scale).astype(np.float32).astype(dtype).astype(np.float64)
    return np.moveaxis((codes * scale).reshape(v.shape), -1, axis)


WIDE = False


def mx_kscale(k):
    if not WIDE:
        return np.ones(k)
    levels = np.array([30, -30])
    if k % 512:
        return np.exp2(np.random.permutation(np.resize(levels, k // 32))).repeat(32)
    a = np.empty((k // 512, 16))
    for p in range(k // 512):
        a[p, :8] = np.random.permutation(np.resize(levels, 8))
        for g in range(8):
            far = levels[np.abs(levels - a[p, g]) >= 10]
            a[p, g + 8] = far[np.random.randint(len(far))]
    return np.exp2(a.ravel()).repeat(32)


def f64(x):
    return np.asarray(x).astype(np.float64)


def striped(idx):
    return np.tile(idx.reshape(-1, 16).T, (8, 1)).astype(np.uint16)


def unstriped(offs):
    return offs[:16].T.reshape(-1).astype(np.int64)


E2M1 = np.array([0.0, 0.5, 1.0, 1.5, 2.0, 3.0, 4.0, 6.0, -0.0, -0.5, -1.0, -1.5, -2.0, -3.0, -4.0, -6.0])


def pack_weight(w, fmt):
    k, n = w.shape
    w = f64(np.asarray(w, np.float32).astype(ml_dtypes.bfloat16)).reshape(k // 32, 32, n)
    amax = np.abs(w).max(1)
    if fmt == "e4m3":
        byte = np.frexp(amax)[1] - 1 + 127 - 7
    else:
        mant, ex = np.frexp(amax / 6.0)
        byte = np.where(mant > 0.5, ex, ex - 1) + 127
    byte = np.clip(np.where(amax > 0, byte, 1), 1, 254)
    scaled = (w * np.exp2(127.0 - byte)[:, None, :]).reshape(k, n).astype(np.float32)
    by_word = np.ascontiguousarray(scaled.reshape(k // 512, 128, 4, n).transpose(0, 1, 3, 2))
    if fmt == "e4m3":
        words = by_word.astype(ml_dtypes.float8_e4m3fn).view(np.uint8)
    else:
        c = by_word.astype(ml_dtypes.float4_e2m1fn).view(np.uint8) & 0xF
        words = (c[..., 0::2] | (c[..., 1::2] << 4)).reshape(k // 512, 128, 2 * n)
    return np.ascontiguousarray(words), np.ascontiguousarray(byte.astype(np.uint8).reshape(k // 512, 16, n))


def unpack_weight(words, scales, fmt):
    g, _, n = scales.shape
    words = np.ascontiguousarray(words).reshape(g, 128, n, -1)
    if fmt == "e4m3":
        vals = words.view(ml_dtypes.float8_e4m3fn).astype(np.float64)
    else:
        nib = np.empty((g, 128, n, 4), np.uint8)
        nib[..., 0::2] = words & 0xF
        nib[..., 1::2] = words >> 4
        vals = E2M1[nib]
    vals = vals * np.repeat(np.exp2(scales.astype(np.float64) - 127.0), 8, axis=1)[..., None]
    return vals.transpose(0, 1, 3, 2).reshape(g * 512, n)


def d_relu(v):
    return (v > 0).astype(np.float64)


K, T, E, C, H, N = 768, 1536, 2, 512, 512, 1024


def by_expert(wq, xq):
    return np.concatenate([wq[e].T @ xq[:, e * C:(e + 1) * C] for e in range(E)], axis=1)


def setup_inputs():
    n = np.random.standard_normal
    s = mx_kscale(N)[:, None]
    u = mx_kscale(H)
    w2 = [pack_weight(m, "e2m1") for m in n((E, N, H)) / np.sqrt(N) / s[None] * u[None, None, :]]
    w1 = [pack_weight(m, "e2m1") for m in n((E, H, K)) / np.sqrt(H) / u[None, :, None]]
    return {
        "dyT": (n((N, T)) * s).astype(np.float32),
        "a": n((H, E * C)).astype(np.float32),
        "w2_words": np.stack([m[0] for m in w2]),
        "w2_scales": np.stack([m[1] for m in w2]),
        "w1_words": np.stack([m[0] for m in w1]),
        "w1_scales": np.stack([m[1] for m in w1]),
        "gate": np.tile(np.random.uniform(0.2, 1.0, E * C), (N, 1)).astype(np.float32),
        "offs": striped(np.random.permutation(T)[:E * C]),
    }


def reference(dyT, a, w2_words, w2_scales, w1_words, w1_scales, gate, offs):
    idx = unstriped(offs)
    w2 = np.stack([unpack_weight(w2_words[e], w2_scales[e], "e2m1") for e in range(E)])
    w1 = np.stack([unpack_weight(w1_words[e], w1_scales[e], "e2m1") for e in range(E)])
    gq = mxq(f64(gate) * f64(dyT)[:, idx], 0, "e5m2")
    dh = by_expert(w2, gq)
    da = dh * d_relu(f64(a))
    dx = by_expert(w1, mxq(da, 0, "e5m2"))
    out = np.zeros((K, T))
    out[:, idx] = dx
    return out

@@ -1,0 +1,148 @@
+from contextlib import ExitStack
+
+import concourse.mybir as mybir
+
+K, T, E, C, H, N = 768, 1536, 2, 512, 512, 1024
+S = E * C
+P = 128
+PACK = 4
+N_PASSES = N // (P * PACK)
+K_BLOCKS = K // P
+
+FLOPS = 2 * S * H * (N + K)
+BYTES = 4 * N * T + 4 * H * S + E * (N * H + H * K) // 2 + E * (N * H + H * K) // 32 + 4 * S + 2 * P * S // 16 + 4 * K * T
+
+F32 = mybir.dt.float32
+BF16 = mybir.dt.bfloat16
+I32 = mybir.dt.int32
+U32 = mybir.dt.uint32
+U16 = mybir.dt.uint16
+U8 = mybir.dt.uint8
+FP4X4 = mybir.dt.float4_e2m1fn_x4
+FP8X4 = mybir.dt.float8_e5m2_x4
+MULT = mybir.AluOpType.mult
+IS_GT = mybir.AluOpType.is_gt
+
+
+def tile_moe_bdx_mlp_relu_kernel(tc, dyT, a, w2_words, w2_scales, w1_words, w1_scales, gate, offs, out):
+    nc = tc.nc
+    with ExitStack() as ctx:
+        keep = ctx.enter_context(tc.tile_pool(name="keep", bufs=1))
+        psum_h = ctx.enter_context(tc.psum_pool(name="psum_h", bufs=4))
+        psum_x = ctx.enter_context(tc.psum_pool(name="psum_x", bufs=4))
+
+        offs_sb = keep.tile([P, S // 16], U16, name="offs_sb")
+        gate_sb = keep.tile([P, S], F32, name="gate_sb")
+        planes = [[keep.tile([P, T], F32, name=f"dy_{s}_{t}") for t in range(PACK)] for s in range(N_PASSES)]
+        a_sb = [keep.tile([P, PACK, C], F32, name=f"a_{e}") for e in range(E)]
+        w2_raw = [keep.tile([P, N_PASSES, 2 * H], U8, name=f"w2_raw_{e}", align_bytes=64) for e in range(E)]
+        w2_sb = [keep.tile([P, N_PASSES, 2 * H], U8, name=f"w2_{e}", align_bytes=64) for e in range(E)]
+        s2_raw = keep.tile([P, E * N_PASSES, H], U8, name="s2_raw", align_bytes=64)
+        s2_sb = [keep.tile([P, N_PASSES, H], U8, name=f"s2_{e}", align_bytes=64) for e in range(E)]
+        w1_sb = keep.tile([P, E, 2 * K], U8, name="w1_sb", align_bytes=64)
+        s1_sb = keep.tile([P, E, K], U8, name="s1_sb", align_bytes=64)
+        windows = [keep.tile([P, T], F32, name=f"window_{b}") for b in range(K_BLOCKS)]
+
+        nc.vector.memset(s2_raw[:].rearrange("p q i -> p (q i)").bitcast(I32), 0)
+        nc.sync.dma_start(offs_sb[:], offs)
+        s2_view = w2_scales.rearrange("e s f i -> f (e s) i")
+        for q in range(4):
+            nc.scalar.dma_start(s2_raw[32 * q : 32 * q + 4, :, :].bitcast(I32), s2_view[4 * q : 4 * q + 4].bitcast(I32))
+        w2_view = w2_words.rearrange("e s p b -> e p s b")
+        nc.scalar.dma_start(w2_raw[0][:].bitcast(I32), w2_view[0].bitcast(I32))
+        nc.sync.dma_start(gate_sb[:], gate[0:P, :])
+        dy_view = dyT.rearrange("(s p t) c -> s t p c", p=P, t=PACK)
+        a_view = a.rearrange("(p t) c -> p t c", t=PACK)
+        for s in range(N_PASSES):
+            for t in range(PACK):
+                nc.sync.dma_start(planes[s][t][:], dy_view[s, t])
+        nc.scalar.dma_start(w2_raw[1][:].bitcast(I32), w2_view[1].bitcast(I32))
+        nc.gpsimd.memset(s1_sb[:].rearrange("p e k -> p (e k)").bitcast(I32), 0)
+        nc.sync.dma_start(a_sb[0][:], a_view[:, :, 0:C])
+        s1_view = w1_scales.rearrange("e s f k -> f (e s) k")
+        for q in range(4):
+            nc.sync.dma_start(s1_sb[32 * q : 32 * q + 4, :, :].bitcast(I32), s1_view[4 * q : 4 * q + 4].bitcast(I32))
+        nc.sync.dma_start(w1_sb[:].bitcast(I32), w1_words.rearrange("e s p b -> p (e s) b").bitcast(I32))
+        nc.sync.dma_start(a_sb[1][:], a_view[:, :, C : 2 * C])
+
+        for b in range(K_BLOCKS):
+            (nc.vector if b < 4 else nc.gpsimd).memset(windows[b][:], 0.0)
+
+        def permute_w2(e):
+            nc.vector.tensor_copy(
+                w2_sb[e][:].rearrange("p s b -> p (s b)").bitcast(U16).rearrange("p (s t m) -> p s t m", s=N_PASSES, t=PACK),
+                w2_raw[e][:].rearrange("p s b -> p (s b)").bitcast(U16).rearrange("p (s m t) -> p s t m", s=N_PASSES, t=PACK),
+            )
+            nc.vector.tensor_copy(
+                s2_sb[e][:].rearrange("p s (t m) -> p s t m", t=PACK),
+                s2_raw[:, N_PASSES * e : N_PASSES * (e + 1), :].rearrange("p s (m t) -> p s t m", t=PACK),
+            )
+
+        permute_w2(0)
+
+        g0 = keep.tile([P, PACK, S], F32, name="g0")
+        gi0 = [keep.tile([P, C, PACK], BF16, name=f"gi0_{e}", align_bytes=64) for e in range(E)]
+        codes = [[keep.tile([P, C], U32, name=f"codes_{s}_{e}", align_bytes=64) for e in range(E)] for s in range(N_PASSES)]
+        scales = [[keep.tile([P, C], U8, name=f"scales_{s}_{e}", align_bytes=64) for e in range(E)] for s in range(N_PASSES)]
+        for t in range(PACK):
+            nc.vector.tensor_tensor(g0[:, t, :], planes[0][t][:].indirect(offs_sb[:]), gate_sb[:], MULT)
+
+        def quantize(grouped, words, bytes_):
+            nc.vector.quantize_mx(out=words[:].bitcast(FP8X4), scales=bytes_[:], in_=grouped[:].rearrange("p c t -> p (c t)"))
+
+        def interleave(grouped, rows):
+            nc.scalar.copy(grouped[:], rows.rearrange("p t c -> p c t"))
+
+        x_sb = [[keep.tile([P, C], F32, name=f"x_{e}_{b}") for b in range(K_BLOCKS)] for e in range(E)]
+        for e in range(E):
+            if e == 1:
+                permute_w2(1)
+            slots = slice(e * C, (e + 1) * C)
+            cols = slice(e * C // 16, (e + 1) * C // 16)
+            g1 = keep.tile([P, PACK, C], F32, name=f"g1_{e}")
+            for t in range(PACK):
+                nc.vector.tensor_tensor(g1[:, t, :], planes[1][t][:].indirect(offs_sb[:, cols]), gate_sb[:, slots], MULT)
+            interleave(gi0[e], g0[:, :, slots])
+            quantize(gi0[e], codes[0][e], scales[0][e])
+            gi1 = keep.tile([P, C, PACK], BF16, name=f"gi1_{e}", align_bytes=64)
+            interleave(gi1, g1[:])
+            quantize(gi1, codes[1][e], scales[1][e])
+
+            da = keep.tile([P, PACK, C], BF16, name=f"da_{e}", align_bytes=64)
+            for t in range(PACK):
+                dh = psum_h.tile([P, C], F32, name="dh")
+                for s in range(N_PASSES):
+                    nc.tensor.matmul_mx(
+                        out=dh[:],
+                        lhsT=w2_sb[e][:, s, 256 * t : 256 * (t + 1)].bitcast(FP4X4),
+                        lhsT_scale=s2_sb[e][:, s, P * t : P * (t + 1)],
+                        rhs=codes[s][e][:].bitcast(FP8X4),
+                        rhs_scale=scales[s][e][:],
+                        start=(s == 0),
+                        stop=(s == N_PASSES - 1),
+                    )
+                nc.vector.scalar_tensor_tensor(da[:, t, :], a_sb[e][:, t, :], 0.0, dh[:], op0=IS_GT, op1=MULT)
+            dai = keep.tile([P, C, PACK], BF16, name=f"dai_{e}", align_bytes=64)
+            interleave(dai, da[:])
+            da_codes = keep.tile([P, C], U32, name=f"da_codes_{e}", align_bytes=64)
+            da_scales = keep.tile([P, C], U8, name=f"da_scales_{e}", align_bytes=64)
+            quantize(dai, da_codes, da_scales)
+            for b in range(K_BLOCKS):
+                dx = psum_x.tile([P, C], F32, name="dx")
+                nc.tensor.matmul_mx(
+                    out=dx[:],
+                    lhsT=w1_sb[:, e, 256 * b : 256 * (b + 1)].bitcast(FP4X4),
+                    lhsT_scale=s1_sb[:, e, P * b : P * (b + 1)],
+                    rhs=da_codes[:].bitcast(FP8X4),
+                    rhs_scale=da_scales[:],
+                    start=True,
+                    stop=True,
+                )
+                nc.scalar.copy(x_sb[e][b][:], dx[:])
+
+        for e in range(E):
+            cols = slice(e * C // 16, (e + 1) * C // 16)
+            for b in range(K_BLOCKS):
+                nc.vector.tensor_copy(windows[b][:].indirect(offs_sb[:, cols]), x_sb[e][b][:])
+                if e == E - 1:
+                    nc.sync.dma_start(out[P * b : P * (b + 1), :], windows[b][:])

@@ -46,18 +46,20 @@ def tile_moe_bdx_mlp_relu_kernel(tc, dyT, a, w2_words, w2_scales, w1_words, w1_s
         nc.vector.memset(s2_raw[:].rearrange("p q i -> p (q i)").bitcast(I32), 0)
         nc.sync.dma_start(offs_sb[:], offs)
         s2_view = w2_scales.rearrange("e s f i -> f (e s) i")
-        for q in range(4):
-            nc.scalar.dma_start(s2_raw[32 * q : 32 * q + 4, :, :].bitcast(I32), s2_view[4 * q : 4 * q + 4].bitcast(I32))
         w2_view = w2_words.rearrange("e s p b -> e p s b")
         nc.scalar.dma_start(w2_raw[0][:].bitcast(I32), w2_view[0].bitcast(I32))
-        nc.sync.dma_start(gate_sb[:], gate[0:P, :])
+        for q in range(4):
+            nc.scalar.dma_start(s2_raw[32 * q : 32 * q + 4, :, :].bitcast(I32), s2_view[4 * q : 4 * q + 4].bitcast(I32))
+        nc.sync.dma_start(gate_sb[:, 0:C], gate[0:P, 0:C])
         dy_view = dyT.rearrange("(s p t) c -> s t p c", p=P, t=PACK)
         a_view = a.rearrange("(p t) c -> p t c", t=PACK)
         for s in range(N_PASSES):
             for t in range(PACK):
                 nc.sync.dma_start(planes[s][t][:], dy_view[s, t])
+                if s == 0 and t == 0:
+                    nc.sync.dma_start(gate_sb[:, C:S], gate[0:P, C:S])
         nc.scalar.dma_start(w2_raw[1][:].bitcast(I32), w2_view[1].bitcast(I32))
-        nc.gpsimd.memset(s1_sb[:].rearrange("p e k -> p (e k)").bitcast(I32), 0)
+        nc.vector.memset(s1_sb[:].rearrange("p e k -> p (e k)").bitcast(I32), 0)
         nc.sync.dma_start(a_sb[0][:], a_view[:, :, 0:C])
         s1_view = w1_scales.rearrange("e s f k -> f (e s) k")
         for q in range(4):
@@ -66,37 +68,46 @@ def tile_moe_bdx_mlp_relu_kernel(tc, dyT, a, w2_words, w2_scales, w1_words, w1_s
         nc.sync.dma_start(a_sb[1][:], a_view[:, :, C : 2 * C])
 
         for b in range(K_BLOCKS):
-            (nc.vector if b < 4 else nc.gpsimd).memset(windows[b][:], 0.0)
+            if b < 3:
+                nc.vector.memset(windows[b][:], 0.0)
+            else:
+                nc.scalar.copy(windows[b][:], windows[0][:])
 
-        def permute_w2(e):
+        def permute_words(e):
             nc.vector.tensor_copy(
                 w2_sb[e][:].rearrange("p s b -> p (s b)").bitcast(U16).rearrange("p (s t m) -> p s t m", s=N_PASSES, t=PACK),
                 w2_raw[e][:].rearrange("p s b -> p (s b)").bitcast(U16).rearrange("p (s m t) -> p s t m", s=N_PASSES, t=PACK),
             )
+
+        def permute_scales(e):
             nc.vector.tensor_copy(
                 s2_sb[e][:].rearrange("p s (t m) -> p s t m", t=PACK),
                 s2_raw[:, N_PASSES * e : N_PASSES * (e + 1), :].rearrange("p s (m t) -> p s t m", t=PACK),
             )
 
-        permute_w2(0)
+        permute_words(0)
 
         g0 = keep.tile([P, PACK, S], F32, name="g0")
         gi0 = [keep.tile([P, C, PACK], BF16, name=f"gi0_{e}", align_bytes=64) for e in range(E)]
         codes = [[keep.tile([P, C], U32, name=f"codes_{s}_{e}", align_bytes=64) for e in range(E)] for s in range(N_PASSES)]
         scales = [[keep.tile([P, C], U8, name=f"scales_{s}_{e}", align_bytes=64) for e in range(E)] for s in range(N_PASSES)]
         for t in range(PACK):
-            nc.vector.tensor_tensor(g0[:, t, :], planes[0][t][:].indirect(offs_sb[:]), gate_sb[:], MULT)
+            for part in (slice(0, C), slice(C, S)) if t == 0 else (slice(0, S),):
+                cols = slice(part.start // 16, part.stop // 16)
+                nc.vector.tensor_tensor(g0[:, t, part], planes[0][t][:].indirect(offs_sb[:, cols]), gate_sb[:, part], MULT)
+        permute_scales(0)
 
         def quantize(grouped, words, bytes_):
             nc.vector.quantize_mx(out=words[:].bitcast(FP8X4), scales=bytes_[:], in_=grouped[:].rearrange("p c t -> p (c t)"))
 
         def interleave(grouped, rows):
-            nc.scalar.copy(grouped[:], rows.rearrange("p t c -> p c t"))
+            nc.scalar.copy(grouped[:].rearrange("p (c i) t -> p c t i", i=4), rows.rearrange("p t (c i) -> p c t i", i=4))
 
         x_sb = [[keep.tile([P, C], F32, name=f"x_{e}_{b}") for b in range(K_BLOCKS)] for e in range(E)]
         for e in range(E):
             if e == 1:
-                permute_w2(1)
+                permute_words(1)
+                permute_scales(1)
             slots = slice(e * C, (e + 1) * C)
             cols = slice(e * C // 16, (e + 1) * C // 16)
             g1 = keep.tile([P, PACK, C], F32, name=f"g1_{e}")

@@ -22,6 +22,8 @@ FP4X4 = mybir.dt.float4_e2m1fn_x4
 FP8X4 = mybir.dt.float8_e5m2_x4
 MULT = mybir.AluOpType.mult
 IS_GT = mybir.AluOpType.is_gt
+SIGN = mybir.ActivationFunctionType.Sign
+RELU = mybir.ActivationFunctionType.Relu
 
 
 def tile_moe_bdx_mlp_relu_kernel(tc, dyT, a, w2_words, w2_scales, w1_words, w1_scales, gate, offs, out):
@@ -38,37 +40,40 @@ def tile_moe_bdx_mlp_relu_kernel(tc, dyT, a, w2_words, w2_scales, w1_words, w1_s
         w2_raw = [keep.tile([P, N_PASSES, 2 * H], U8, name=f"w2_raw_{e}", align_bytes=64) for e in range(E)]
         w2_sb = [keep.tile([P, N_PASSES, 2 * H], U8, name=f"w2_{e}", align_bytes=64) for e in range(E)]
         s2_raw = keep.tile([P, E * N_PASSES, H], U8, name="s2_raw", align_bytes=64)
-        s2_sb = [keep.tile([P, N_PASSES, H], U8, name=f"s2_{e}", align_bytes=64) for e in range(E)]
+        s2_sb = keep.tile([P, E * N_PASSES, H], U8, name="s2_sb", align_bytes=64)
         w1_sb = keep.tile([P, E, 2 * K], U8, name="w1_sb", align_bytes=64)
         s1_sb = keep.tile([P, E, K], U8, name="s1_sb", align_bytes=64)
         windows = [keep.tile([P, T], F32, name=f"window_{b}") for b in range(K_BLOCKS)]
+        g0 = keep.tile([P, PACK, S], F32, name="g0")
+        codes = [[keep.tile([P, C], U32, name=f"codes_{s}_{e}", align_bytes=64) for e in range(E)] for s in range(N_PASSES)]
+        scales = [[keep.tile([P, C], U8, name=f"scales_{s}_{e}", align_bytes=64) for e in range(E)] for s in range(N_PASSES)]
 
-        nc.vector.memset(s2_raw[:].rearrange("p q i -> p (q i)").bitcast(I32), 0)
-        nc.sync.dma_start(offs_sb[:], offs)
         s2_view = w2_scales.rearrange("e s f i -> f (e s) i")
+        s1_view = w1_scales.rearrange("e s f k -> f (e s) k")
         w2_view = w2_words.rearrange("e s p b -> e p s b")
-        nc.scalar.dma_start(w2_raw[0][:].bitcast(I32), w2_view[0].bitcast(I32))
-        for q in range(4):
-            nc.scalar.dma_start(s2_raw[32 * q : 32 * q + 4, :, :].bitcast(I32), s2_view[4 * q : 4 * q + 4].bitcast(I32))
-        nc.sync.dma_start(gate_sb[:, 0:C], gate[0:P, 0:C])
         dy_view = dyT.rearrange("(s p t) c -> s t p c", p=P, t=PACK)
         a_view = a.rearrange("(p t) c -> p t c", t=PACK)
+        nc.vector.memset(s2_raw[:].rearrange("p q i -> p (q i)").bitcast(I32), 0)
+        nc.vector.memset(s1_sb[:].rearrange("p e k -> p (e k)").bitcast(I32), 0)
+        nc.sync.dma_start(offs_sb[:], offs)
+        for q in range(4):
+            nc.sync.dma_start(s2_raw[32 * q : 32 * q + 4, :, :].bitcast(I32), s2_view[4 * q : 4 * q + 4].bitcast(I32))
+        nc.sync.dma_start(w2_raw[0][:].bitcast(I32), w2_view[0].bitcast(I32))
+        nc.sync.dma_start(gate_sb[:, 0:C], gate[0:P, 0:C])
         for s in range(N_PASSES):
             for t in range(PACK):
                 nc.sync.dma_start(planes[s][t][:], dy_view[s, t])
                 if s == 0 and t == 0:
                     nc.sync.dma_start(gate_sb[:, C:S], gate[0:P, C:S])
         nc.scalar.dma_start(w2_raw[1][:].bitcast(I32), w2_view[1].bitcast(I32))
-        nc.vector.memset(s1_sb[:].rearrange("p e k -> p (e k)").bitcast(I32), 0)
         nc.sync.dma_start(a_sb[0][:], a_view[:, :, 0:C])
-        s1_view = w1_scales.rearrange("e s f k -> f (e s) k")
         for q in range(4):
             nc.sync.dma_start(s1_sb[32 * q : 32 * q + 4, :, :].bitcast(I32), s1_view[4 * q : 4 * q + 4].bitcast(I32))
         nc.sync.dma_start(w1_sb[:].bitcast(I32), w1_words.rearrange("e s p b -> p (e s) b").bitcast(I32))
         nc.sync.dma_start(a_sb[1][:], a_view[:, :, C : 2 * C])
 
         for b in range(K_BLOCKS):
-            if b < 3:
+            if b < 1:
                 nc.vector.memset(windows[b][:], 0.0)
             else:
                 nc.scalar.copy(windows[b][:], windows[0][:])
@@ -79,81 +84,100 @@ def tile_moe_bdx_mlp_relu_kernel(tc, dyT, a, w2_words, w2_scales, w1_words, w1_s
                 w2_raw[e][:].rearrange("p s b -> p (s b)").bitcast(U16).rearrange("p (s m t) -> p s t m", s=N_PASSES, t=PACK),
             )
 
-        def permute_scales(e):
+        def permute_scales():
             nc.vector.tensor_copy(
-                s2_sb[e][:].rearrange("p s (t m) -> p s t m", t=PACK),
-                s2_raw[:, N_PASSES * e : N_PASSES * (e + 1), :].rearrange("p s (m t) -> p s t m", t=PACK),
+                s2_sb[:].rearrange("p q (t m) -> p q t m", t=PACK),
+                s2_raw[:].rearrange("p q (m t) -> p q t m", t=PACK),
             )
 
-        permute_words(0)
-
-        g0 = keep.tile([P, PACK, S], F32, name="g0")
-        gi0 = [keep.tile([P, C, PACK], BF16, name=f"gi0_{e}", align_bytes=64) for e in range(E)]
-        codes = [[keep.tile([P, C], U32, name=f"codes_{s}_{e}", align_bytes=64) for e in range(E)] for s in range(N_PASSES)]
-        scales = [[keep.tile([P, C], U8, name=f"scales_{s}_{e}", align_bytes=64) for e in range(E)] for s in range(N_PASSES)]
-        for t in range(PACK):
-            for part in (slice(0, C), slice(C, S)) if t == 0 else (slice(0, S),):
-                cols = slice(part.start // 16, part.stop // 16)
-                nc.vector.tensor_tensor(g0[:, t, part], planes[0][t][:].indirect(offs_sb[:, cols]), gate_sb[:, part], MULT)
-        permute_scales(0)
-
-        def quantize(grouped, words, bytes_):
-            nc.vector.quantize_mx(out=words[:].bitcast(FP8X4), scales=bytes_[:], in_=grouped[:].rearrange("p c t -> p (c t)"))
+        def quantize(grouped, words, scale_bytes):
+            nc.vector.quantize_mx(out=words[:].bitcast(FP8X4), scales=scale_bytes[:], in_=grouped[:].rearrange("p c t -> p (c t)"))
 
         def interleave(grouped, rows):
             nc.scalar.copy(grouped[:].rearrange("p (c i) t -> p c t i", i=4), rows.rearrange("p t (c i) -> p c t i", i=4))
 
-        x_sb = [[keep.tile([P, C], F32, name=f"x_{e}_{b}") for b in range(K_BLOCKS)] for e in range(E)]
-        for e in range(E):
-            if e == 1:
-                permute_words(1)
-                permute_scales(1)
-            slots = slice(e * C, (e + 1) * C)
-            cols = slice(e * C // 16, (e + 1) * C // 16)
+        def gather(s, t, e0, e1, rows):
+            slots = slice(e0 * C, e1 * C)
+            cols = slice(slots.start // 16, slots.stop // 16)
+            nc.vector.tensor_tensor(rows, planes[s][t][:].indirect(offs_sb[:, cols]), gate_sb[:, slots], MULT)
+
+        permute_scales()
+        permute_words(0)
+        gather(0, 0, 0, 1, g0[:, 0, 0:C])
+        gather(0, 0, 1, 2, g0[:, 0, C:S])
+        for t in range(1, PACK):
+            gather(0, t, 0, 2, g0[:, t, :])
+
+
+        def slot_gradients(e):
             g1 = keep.tile([P, PACK, C], F32, name=f"g1_{e}")
             for t in range(PACK):
-                nc.vector.tensor_tensor(g1[:, t, :], planes[1][t][:].indirect(offs_sb[:, cols]), gate_sb[:, slots], MULT)
-            interleave(gi0[e], g0[:, :, slots])
-            quantize(gi0[e], codes[0][e], scales[0][e])
+                gather(1, t, e, e + 1, g1[:, t, :])
+            gi0 = keep.tile([P, C, PACK], BF16, name=f"gi0_{e}", align_bytes=64)
+            interleave(gi0, g0[:, :, e * C : (e + 1) * C])
+            quantize(gi0, codes[0][e], scales[0][e])
             gi1 = keep.tile([P, C, PACK], BF16, name=f"gi1_{e}", align_bytes=64)
             interleave(gi1, g1[:])
             quantize(gi1, codes[1][e], scales[1][e])
 
-            da = keep.tile([P, PACK, C], BF16, name=f"da_{e}", align_bytes=64)
-            for t in range(PACK):
-                dh = psum_h.tile([P, C], F32, name="dh")
-                for s in range(N_PASSES):
-                    nc.tensor.matmul_mx(
-                        out=dh[:],
-                        lhsT=w2_sb[e][:, s, 256 * t : 256 * (t + 1)].bitcast(FP4X4),
-                        lhsT_scale=s2_sb[e][:, s, P * t : P * (t + 1)],
-                        rhs=codes[s][e][:].bitcast(FP8X4),
-                        rhs_scale=scales[s][e][:],
-                        start=(s == 0),
-                        stop=(s == N_PASSES - 1),
-                    )
-                nc.vector.scalar_tensor_tensor(da[:, t, :], a_sb[e][:, t, :], 0.0, dh[:], op0=IS_GT, op1=MULT)
-            dai = keep.tile([P, C, PACK], BF16, name=f"dai_{e}", align_bytes=64)
-            interleave(dai, da[:])
-            da_codes = keep.tile([P, C], U32, name=f"da_codes_{e}", align_bytes=64)
-            da_scales = keep.tile([P, C], U8, name=f"da_scales_{e}", align_bytes=64)
-            quantize(dai, da_codes, da_scales)
-            for b in range(K_BLOCKS):
-                dx = psum_x.tile([P, C], F32, name="dx")
+        def first_product(e, t):
+            dh = psum_h.tile([P, C], F32, name="dh")
+            for s in range(N_PASSES):
                 nc.tensor.matmul_mx(
-                    out=dx[:],
-                    lhsT=w1_sb[:, e, 256 * b : 256 * (b + 1)].bitcast(FP4X4),
-                    lhsT_scale=s1_sb[:, e, P * b : P * (b + 1)],
-                    rhs=da_codes[:].bitcast(FP8X4),
-                    rhs_scale=da_scales[:],
-                    start=True,
-                    stop=True,
+                    out=dh[:],
+                    lhsT=w2_sb[e][:, s, 256 * t : 256 * (t + 1)].bitcast(FP4X4),
+                    lhsT_scale=s2_sb[:, N_PASSES * e + s, P * t : P * (t + 1)],
+                    rhs=codes[s][e][:].bitcast(FP8X4),
+                    rhs_scale=scales[s][e][:],
+                    start=(s == 0),
+                    stop=(s == N_PASSES - 1),
                 )
-                nc.scalar.copy(x_sb[e][b][:], dx[:])
+            return dh
+
+        def second_product(e, b, pool):
+            dx = pool.tile([P, C], F32, name="dx" if pool is psum_x else "dh")
+            nc.tensor.matmul_mx(
+                out=dx[:],
+                lhsT=w1_sb[:, e, 256 * b : 256 * (b + 1)].bitcast(FP4X4),
+                lhsT_scale=s1_sb[:, e, P * b : P * (b + 1)],
+                rhs=da_codes[e][:].bitcast(FP8X4),
+                rhs_scale=da_scales[e][:],
+                start=True,
+                stop=True,
+            )
+            x = keep.tile([P, C], F32, name=f"x_{e}_{b}", tag="late" if (e, b) == (0, 5) else f"x_{e}_{b}", align_bytes=64)
+            nc.scalar.copy(x[:], dx[:])
+            x_sb[(e, b)] = x
+
+        da_codes = [keep.tile([P, C], U32, name=f"da_codes_{e}", align_bytes=64) for e in range(E)]
+        da_scales = [keep.tile([P, C], U8, name=f"da_scales_{e}", align_bytes=64) for e in range(E)]
+        dai = [keep.tile([P, C, PACK], BF16, name=f"dai_{e}", align_bytes=64) for e in range(E)]
+        x_sb = {}
+
+        slot_gradients(0)
+        da0 = keep.tile([P, PACK, C], BF16, name="da0", align_bytes=64)
+        for t in range(PACK):
+            dh = first_product(0, t)
+            nc.vector.scalar_tensor_tensor(da0[:, t, :], a_sb[0][:, t, :], 0.0, dh[:], op0=IS_GT, op1=MULT)
+        interleave(dai[0], da0[:])
+        quantize(dai[0], da_codes[0], da_scales[0])
+        for b in range(5):
+            second_product(0, b, psum_x)
+
+        permute_words(1)
+        slot_gradients(1)
+        da1 = keep.tile([P, PACK, C], BF16, name="da1", tag="late", align_bytes=64)
+        for t in range(PACK):
+            dh = first_product(1, t)
+            nc.vector.scalar_tensor_tensor(da1[:, t, :], a_sb[1][:, t, :], 0.0, dh[:], op0=IS_GT, op1=MULT)
+        interleave(dai[1], da1[:])
+        quantize(dai[1], da_codes[1], da_scales[1])
+        second_product(0, 5, psum_x)
+        for b in range(K_BLOCKS):
+            second_product(1, b, psum_x)
 
         for e in range(E):
-            cols = slice(e * C // 16, (e + 1) * C // 16)
             for b in range(K_BLOCKS):
-                nc.vector.tensor_copy(windows[b][:].indirect(offs_sb[:, cols]), x_sb[e][b][:])
+                nc.vector.tensor_copy(windows[b][:].indirect(offs_sb[:, 32 * e : 32 * e + 32]), x_sb[(e, b)][:])
                 if e == E - 1:
                     nc.sync.dma_start(out[P * b : P * (b + 1), :], windows[b][:])

@@ -8,6 +8,7 @@ P = 128
 PACK = 4
 N_PASSES = N // (P * PACK)
 K_BLOCKS = K // P
+JOINT = 2
 
 FLOPS = 2 * S * H * (N + K)
 BYTES = 4 * N * T + 4 * H * S + E * (N * H + H * K) // 2 + E * (N * H + H * K) // 32 + 4 * S + 2 * P * S // 16 + 4 * K * T
@@ -55,9 +56,9 @@ def tile_moe_bdx_mlp_relu_kernel(tc, dyT, a, w2_words, w2_scales, w1_words, w1_s
         a_view = a.rearrange("(p t) c -> p t c", t=PACK)
         nc.vector.memset(s2_raw[:].rearrange("p q i -> p (q i)").bitcast(I32), 0)
         nc.vector.memset(s1_sb[:].rearrange("p e k -> p (e k)").bitcast(I32), 0)
-        nc.sync.dma_start(offs_sb[:], offs)
         for q in range(4):
             nc.sync.dma_start(s2_raw[32 * q : 32 * q + 4, :, :].bitcast(I32), s2_view[4 * q : 4 * q + 4].bitcast(I32))
+        nc.sync.dma_start(offs_sb[:], offs)
         nc.sync.dma_start(w2_raw[0][:].bitcast(I32), w2_view[0].bitcast(I32))
         nc.sync.dma_start(gate_sb[:, 0:C], gate[0:P, 0:C])
         for s in range(N_PASSES):
@@ -65,7 +66,7 @@ def tile_moe_bdx_mlp_relu_kernel(tc, dyT, a, w2_words, w2_scales, w1_words, w1_s
                 nc.sync.dma_start(planes[s][t][:], dy_view[s, t])
                 if s == 0 and t == 0:
                     nc.sync.dma_start(gate_sb[:, C:S], gate[0:P, C:S])
-        nc.scalar.dma_start(w2_raw[1][:].bitcast(I32), w2_view[1].bitcast(I32))
+        nc.sync.dma_start(w2_raw[1][:].bitcast(I32), w2_view[1].bitcast(I32))
         nc.sync.dma_start(a_sb[0][:], a_view[:, :, 0:C])
         for q in range(4):
             nc.sync.dma_start(s1_sb[32 * q : 32 * q + 4, :, :].bitcast(I32), s1_view[4 * q : 4 * q + 4].bitcast(I32))
@@ -105,11 +106,13 @@ def tile_moe_bdx_mlp_relu_kernel(tc, dyT, a, w2_words, w2_scales, w1_words, w1_s
         permute_words(0)
         gather(0, 0, 0, 1, g0[:, 0, 0:C])
         gather(0, 0, 1, 2, g0[:, 0, C:S])
-        for t in range(1, PACK):
+        for t in range(1, JOINT):
             gather(0, t, 0, 2, g0[:, t, :])
 
 
         def slot_gradients(e):
+            for t in range(JOINT, PACK):
+                gather(0, t, e, e + 1, g0[:, t, e * C : (e + 1) * C])
             g1 = keep.tile([P, PACK, C], F32, name=f"g1_{e}")
             for t in range(PACK):
                 gather(1, t, e, e + 1, g1[:, t, :])

from contextlib import ExitStack

import concourse.mybir as mybir

K, T, E, C, H, N = 768, 1536, 2, 512, 512, 1024
S = E * C
P = 128
PACK = 4
N_PASSES = N // (P * PACK)
K_BLOCKS = K // P
JOINT = 2

FLOPS = 2 * S * H * (N + K)
BYTES = 4 * N * T + 4 * H * S + E * (N * H + H * K) // 2 + E * (N * H + H * K) // 32 + 4 * S + 2 * P * S // 16 + 4 * K * T

F32 = mybir.dt.float32
BF16 = mybir.dt.bfloat16
I32 = mybir.dt.int32
U32 = mybir.dt.uint32
U16 = mybir.dt.uint16
U8 = mybir.dt.uint8
FP4X4 = mybir.dt.float4_e2m1fn_x4
FP8X4 = mybir.dt.float8_e5m2_x4
MULT = mybir.AluOpType.mult
IS_GT = mybir.AluOpType.is_gt
SIGN = mybir.ActivationFunctionType.Sign
RELU = mybir.ActivationFunctionType.Relu


def tile_moe_bdx_mlp_relu_kernel(tc, dyT, a, w2_words, w2_scales, w1_words, w1_scales, gate, offs, out):
    nc = tc.nc
    with ExitStack() as ctx:
        keep = ctx.enter_context(tc.tile_pool(name="keep", bufs=1))
        psum_h = ctx.enter_context(tc.psum_pool(name="psum_h", bufs=4))
        psum_x = ctx.enter_context(tc.psum_pool(name="psum_x", bufs=4))

        offs_sb = keep.tile([P, S // 16], U16, name="offs_sb")
        gate_sb = keep.tile([P, S], F32, name="gate_sb")
        planes = [[keep.tile([P, T], F32, name=f"dy_{s}_{t}") for t in range(PACK)] for s in range(N_PASSES)]
        a_sb = [keep.tile([P, PACK, C], F32, name=f"a_{e}") for e in range(E)]
        w2_raw = [keep.tile([P, N_PASSES, 2 * H], U8, name=f"w2_raw_{e}", align_bytes=64) for e in range(E)]
        w2_sb = [keep.tile([P, N_PASSES, 2 * H], U8, name=f"w2_{e}", align_bytes=64) for e in range(E)]
        s2_raw = keep.tile([P, E * N_PASSES, H], U8, name="s2_raw", align_bytes=64)
        s2_sb = keep.tile([P, E * N_PASSES, H], U8, name="s2_sb", align_bytes=64)
        w1_sb = keep.tile([P, E, 2 * K], U8, name="w1_sb", align_bytes=64)
        s1_sb = keep.tile([P, E, K], U8, name="s1_sb", align_bytes=64)
        windows = [keep.tile([P, T], F32, name=f"window_{b}") for b in range(K_BLOCKS)]
        g0 = keep.tile([P, PACK, S], F32, name="g0")
        codes = [[keep.tile([P, C], U32, name=f"codes_{s}_{e}", align_bytes=64) for e in range(E)] for s in range(N_PASSES)]
        scales = [[keep.tile([P, C], U8, name=f"scales_{s}_{e}", align_bytes=64) for e in range(E)] for s in range(N_PASSES)]

        s2_view = w2_scales.rearrange("e s f i -> f (e s) i")
        s1_view = w1_scales.rearrange("e s f k -> f (e s) k")
        w2_view = w2_words.rearrange("e s p b -> e p s b")
        dy_view = dyT.rearrange("(s p t) c -> s t p c", p=P, t=PACK)
        a_view = a.rearrange("(p t) c -> p t c", t=PACK)
        nc.vector.memset(s2_raw[:].rearrange("p q i -> p (q i)").bitcast(I32), 0)
        nc.vector.memset(s1_sb[:].rearrange("p e k -> p (e k)").bitcast(I32), 0)
        for q in range(4):
            nc.sync.dma_start(s2_raw[32 * q : 32 * q + 4, :, :].bitcast(I32), s2_view[4 * q : 4 * q + 4].bitcast(I32))
        nc.sync.dma_start(offs_sb[:], offs)
        nc.sync.dma_start(w2_raw[0][:].bitcast(I32), w2_view[0].bitcast(I32))
        nc.sync.dma_start(gate_sb[:, 0:C], gate[0:P, 0:C])
        for s in range(N_PASSES):
            for t in range(PACK):
                nc.sync.dma_start(planes[s][t][:], dy_view[s, t])
                if s == 0 and t == 0:
                    nc.sync.dma_start(gate_sb[:, C:S], gate[0:P, C:S])
        nc.sync.dma_start(w2_raw[1][:].bitcast(I32), w2_view[1].bitcast(I32))
        nc.sync.dma_start(a_sb[0][:], a_view[:, :, 0:C])
        for q in range(4):
            nc.sync.dma_start(s1_sb[32 * q : 32 * q + 4, :, :].bitcast(I32), s1_view[4 * q : 4 * q + 4].bitcast(I32))
        nc.sync.dma_start(w1_sb[:].bitcast(I32), w1_words.rearrange("e s p b -> p (e s) b").bitcast(I32))
        nc.sync.dma_start(a_sb[1][:], a_view[:, :, C : 2 * C])

        for b in range(K_BLOCKS):
            if b < 1:
                nc.vector.memset(windows[b][:], 0.0)
            else:
                nc.scalar.copy(windows[b][:], windows[0][:])

        def permute_words(e):
            nc.vector.tensor_copy(
                w2_sb[e][:].rearrange("p s b -> p (s b)").bitcast(U16).rearrange("p (s t m) -> p s t m", s=N_PASSES, t=PACK),
                w2_raw[e][:].rearrange("p s b -> p (s b)").bitcast(U16).rearrange("p (s m t) -> p s t m", s=N_PASSES, t=PACK),
            )

        def permute_scales():
            nc.vector.tensor_copy(
                s2_sb[:].rearrange("p q (t m) -> p q t m", t=PACK),
                s2_raw[:].rearrange("p q (m t) -> p q t m", t=PACK),
            )

        def quantize(grouped, words, scale_bytes):
            nc.vector.quantize_mx(out=words[:].bitcast(FP8X4), scales=scale_bytes[:], in_=grouped[:].rearrange("p c t -> p (c t)"))

        def interleave(grouped, rows):
            nc.scalar.copy(grouped[:].rearrange("p (c i) t -> p c t i", i=4), rows.rearrange("p t (c i) -> p c t i", i=4))

        def gather(s, t, e0, e1, rows):
            slots = slice(e0 * C, e1 * C)
            cols = slice(slots.start // 16, slots.stop // 16)
            nc.vector.tensor_tensor(rows, planes[s][t][:].indirect(offs_sb[:, cols]), gate_sb[:, slots], MULT)

        permute_scales()
        permute_words(0)
        gather(0, 0, 0, 1, g0[:, 0, 0:C])
        gather(0, 0, 1, 2, g0[:, 0, C:S])
        for t in range(1, JOINT):
            gather(0, t, 0, 2, g0[:, t, :])


        def slot_gradients(e):
            for t in range(JOINT, PACK):
                gather(0, t, e, e + 1, g0[:, t, e * C : (e + 1) * C])
            g1 = keep.tile([P, PACK, C], F32, name=f"g1_{e}")
            for t in range(PACK):
                gather(1, t, e, e + 1, g1[:, t, :])
            gi0 = keep.tile([P, C, PACK], BF16, name=f"gi0_{e}", align_bytes=64)
            interleave(gi0, g0[:, :, e * C : (e + 1) * C])
            quantize(gi0, codes[0][e], scales[0][e])
            gi1 = keep.tile([P, C, PACK], BF16, name=f"gi1_{e}", align_bytes=64)
            interleave(gi1, g1[:])
            quantize(gi1, codes[1][e], scales[1][e])

        def first_product(e, t):
            dh = psum_h.tile([P, C], F32, name="dh")
            for s in range(N_PASSES):
                nc.tensor.matmul_mx(
                    out=dh[:],
                    lhsT=w2_sb[e][:, s, 256 * t : 256 * (t + 1)].bitcast(FP4X4),
                    lhsT_scale=s2_sb[:, N_PASSES * e + s, P * t : P * (t + 1)],
                    rhs=codes[s][e][:].bitcast(FP8X4),
                    rhs_scale=scales[s][e][:],
                    start=(s == 0),
                    stop=(s == N_PASSES - 1),
                )
            return dh

        def second_product(e, b, pool):
            dx = pool.tile([P, C], F32, name="dx" if pool is psum_x else "dh")
            nc.tensor.matmul_mx(
                out=dx[:],
                lhsT=w1_sb[:, e, 256 * b : 256 * (b + 1)].bitcast(FP4X4),
                lhsT_scale=s1_sb[:, e, P * b : P * (b + 1)],
                rhs=da_codes[e][:].bitcast(FP8X4),
                rhs_scale=da_scales[e][:],
                start=True,
                stop=True,
            )
            x = keep.tile([P, C], F32, name=f"x_{e}_{b}", tag="late" if (e, b) == (0, 5) else f"x_{e}_{b}", align_bytes=64)
            nc.scalar.copy(x[:], dx[:])
            x_sb[(e, b)] = x

        da_codes = [keep.tile([P, C], U32, name=f"da_codes_{e}", align_bytes=64) for e in range(E)]
        da_scales = [keep.tile([P, C], U8, name=f"da_scales_{e}", align_bytes=64) for e in range(E)]
        dai = [keep.tile([P, C, PACK], BF16, name=f"dai_{e}", align_bytes=64) for e in range(E)]
        x_sb = {}

        slot_gradients(0)
        da0 = keep.tile([P, PACK, C], BF16, name="da0", align_bytes=64)
        for t in range(PACK):
            dh = first_product(0, t)
            nc.vector.scalar_tensor_tensor(da0[:, t, :], a_sb[0][:, t, :], 0.0, dh[:], op0=IS_GT, op1=MULT)
        interleave(dai[0], da0[:])
        quantize(dai[0], da_codes[0], da_scales[0])
        for b in range(5):
            second_product(0, b, psum_x)

        permute_words(1)
        slot_gradients(1)
        da1 = keep.tile([P, PACK, C], BF16, name="da1", tag="late", align_bytes=64)
        for t in range(PACK):
            dh = first_product(1, t)
            nc.vector.scalar_tensor_tensor(da1[:, t, :], a_sb[1][:, t, :], 0.0, dh[:], op0=IS_GT, op1=MULT)
        interleave(dai[1], da1[:])
        quantize(dai[1], da_codes[1], da_scales[1])
        second_product(0, 5, psum_x)
        for b in range(K_BLOCKS):
            second_product(1, b, psum_x)

        for e in range(E):
            for b in range(K_BLOCKS):
                nc.vector.tensor_copy(windows[b][:].indirect(offs_sb[:, 32 * e : 32 * e + 32]), x_sb[(e, b)][:])
                if e == E - 1:
                    nc.sync.dma_start(out[P * b : P * (b + 1), :], windows[b][:])
